import numpy as np
import ml_dtypes


def mxq(x, axis, fmt="e4m3"):
    dtype, down = {"e4m3": (ml_dtypes.float8_e4m3fn, 7), "e5m2": (ml_dtypes.float8_e5m2, 14)}[fmt]
    v = np.moveaxis(np.asarray(x, np.float32).astype(ml_dtypes.bfloat16).astype(np.float64), axis, -1)
    blocks = v.reshape(v.shape[:-1] + (-1, 32))
    amax = np.abs(blocks).max(-1, keepdims=True)
    byte = np.maximum(np.where(amax > 0, np.frexp(amax)[1] - 1 + 127, 0) - down, 1)
    scale = np.exp2(byte - 127.0)
    codes = (blocks / scale).astype(np.float32).astype(dtype).astype(np.float64)
    return np.moveaxis((codes * scale).reshape(v.shape), -1, axis)


WIDE = False


def mx_kscale(k):
    if not WIDE:
        return np.ones(k)
    levels = np.array([10, -10, 5, -5, 0])
    if k % 512:
        return np.exp2(np.random.permutation(np.resize(levels, k // 32))).repeat(32)
    a = np.empty((k // 512, 16))
    for p in range(k // 512):
        a[p, :8] = np.random.permutation(np.resize(levels, 8))
        for g in range(8):
            far = levels[np.abs(levels - a[p, g]) >= 10]
            a[p, g + 8] = far[np.random.randint(len(far))]
    return np.exp2(a.ravel()).repeat(32)


def f64(x):
    return np.asarray(x).astype(np.float64)


def striped(idx):
    return np.tile(idx.reshape(-1, 16).T, (8, 1)).astype(np.uint16)


def unstriped(offs):
    return offs[:16].T.reshape(-1).astype(np.int64)


def striped8(idx):
    return np.concatenate([x.reshape(-1, 16).T for x in idx]).astype(np.uint16)


def runs(offs, k):
    lists = np.stack([offs[16 * r : 16 * r + 16].T.reshape(-1) for r in range(8)]).astype(np.int64)
    return lists[np.arange(k) % 512 // 64]


def pack_weight(w):
    k, n = w.shape
    w = f64(np.asarray(w, np.float32).astype(ml_dtypes.bfloat16)).reshape(k // 32, 32, n)
    amax = np.abs(w).max(1)
    byte = np.clip(np.where(amax > 0, np.frexp(amax)[1] - 1 + 127 - 7, 1), 1, 254)
    scaled = (w * np.exp2(127.0 - byte)[:, None, :]).reshape(k, n).astype(np.float32)
    words = np.ascontiguousarray(scaled.reshape(k // 512, 128, 4, n).transpose(0, 1, 3, 2)).astype(ml_dtypes.float8_e4m3fn).view(np.uint8)
    return words, np.ascontiguousarray(byte.astype(np.uint8).reshape(k // 512, 16, n))


def unpack_weight(words, scales):
    g, p, n, _ = words.shape
    vals = np.ascontiguousarray(words).view(ml_dtypes.float8_e4m3fn).astype(np.float64) * np.repeat(np.exp2(scales.astype(np.float64) - 127.0), 8, axis=1)[..., None]
    return vals.transpose(0, 1, 3, 2).reshape(g * 512, n)

def planes(y):
    n, m = y.shape
    v = y.astype(np.float32).astype(ml_dtypes.bfloat16).astype(np.float64).reshape(n // 32, 32, m)
    top = np.abs(v).max(1)
    byte = np.clip(np.where(top > 0, np.frexp(top)[1] - 1 + 127 - 7, 1), 1, 254)
    codes = (v * np.exp2(127.0 - byte)[:, None, :]).reshape(n, m).astype(np.float32).astype(ml_dtypes.float8_e4m3fn).view(np.uint8)
    words = codes.reshape(n // 512, 128, 4, m).transpose(0, 1, 3, 2)
    return np.ascontiguousarray(words), np.ascontiguousarray(byte.astype(np.uint8).reshape(n // 512, 16, m))


K, T, S, G, H, U = 512, 1024, 512, 2048, 512, 1024


def setup_inputs():
    n = np.random.standard_normal
    s = mx_kscale(K)[:, None]
    packed_xT = pack_weight(n((K, T)) * s)
    packed_dT = pack_weight(n((K, G)) / s)
    return {
        "x_words": packed_xT[0],
        "x_scales": packed_xT[1],
        "d_words": packed_dT[0],
        "d_scales": packed_dT[1],
        "mem": n((H, U)).astype(np.float32),
        "gs": (np.random.uniform(0.5, 1.5, (K, 1)) * s).astype(np.float32),
        "offs": striped(np.random.permutation(T)[:S]),
        "k1": striped8(np.random.randint(0, G, (8, H))),
        "n1": striped8(np.stack([np.random.permutation(U)[:S] for _ in range(8)])),
        "n2": striped8(np.stack([np.random.permutation(U) for _ in range(8)])),
        "k2": striped8(np.random.randint(0, G, (8, H))),
        "n3": striped8(np.stack([np.random.permutation(U) for _ in range(8)])),
        "n4": striped8(np.stack([np.random.permutation(U) for _ in range(8)])),
    }


def reference(x_words, x_scales, d_words, d_scales, mem, gs, offs, k1, n1, n2, k2, n3, n4):
    d_k2 = unpack_weight(d_words, d_scales)[np.arange(K)[:, None], runs(k2, K)]
    d_k1 = unpack_weight(d_words, d_scales)[np.arange(K)[:, None], runs(k1, K)]
    xq = unpack_weight(x_words, x_scales)[:, unstriped(offs)]
    h = 0.0625 * (d_k1.T @ xq)
    pg = f64(mem).copy()
    pg[np.arange(H)[:, None], runs(n1, H)] = h
    z = f64(gs) * (pg - (0.5 * (pg[np.arange(H)[:, None], runs(n2, H)])))
    h2 = 0.0625 * ((d_k2.T @ mxq(z, 0, "e4m3")))
    out_0 = h2[np.arange(H)[:, None], runs(n3, H)] - (h2[np.arange(H)[:, None], runs(n4, H)])
    return (out_0,) + planes(out_0)

@@ -1,0 +1,199 @@
+from contextlib import ExitStack
+
+import concourse.mybir as mybir
+
+K, T, S, G, H, U = 512, 1024, 512, 2048, 512, 1024
+FLOPS = 2 * K * H * S + 2 * K * H * U
+
+F32 = mybir.dt.float32
+BF16 = mybir.dt.bfloat16
+I32 = mybir.dt.int32
+U32 = mybir.dt.uint32
+U16 = mybir.dt.uint16
+U8 = mybir.dt.uint8
+FP8X4 = mybir.dt.float8_e4m3fn_x4
+COPY = mybir.ActivationFunctionType.Copy
+ADD = mybir.AluOpType.add
+SUBTRACT = mybir.AluOpType.subtract
+
+P = 128
+PACK = 4
+PER_COL = 16
+PIECES = [(0, 512), (512, 256), (768, 256)]
+
+
+def tile_picked_codepagemgap_none_po_kernel(
+    tc, x_words, x_scales, d_words, d_scales, mem, gs, offs, k1, n1, n2, k2, n3, n4, out_0, out_1, out_2
+):
+    nc = tc.nc
+    with ExitStack() as ctx:
+        lists = ctx.enter_context(tc.tile_pool(name="lists", bufs=1))
+        keep = ctx.enter_context(tc.tile_pool(name="keep", bufs=1))
+        psum = ctx.enter_context(tc.psum_pool(name="psum", bufs=8))
+
+        def load_list(name, src):
+            tile = lists.tile(list(src.shape), U16, name=name)
+            nc.sync.dma_start(tile[:], src)
+            return tile
+
+        def sb(name, shape, dtype, tag=None):
+            return keep.tile(shape, dtype, name=name, tag=tag or name, align_bytes=64)
+
+        def load_scale_rows(tile, src):
+            rows = src[0].bitcast(I32)
+            nc.sync.dma_start(tile[:].bitcast(I32), rows.unsqueeze(1).broadcast_to([16, 8, rows.shape[1]]))
+
+        def load_words(tile, src):
+            nc.sync.dma_start(tile[:].bitcast(I32), src[0].rearrange("p c r -> p (c r)").bitcast(I32))
+
+        def place_scale_rows(queue, dst, src):
+            for r in range(4):
+                queue.dma_start(dst[r:P:32, :].bitcast(I32), src[8 * r : P : 32, :].bitcast(I32))
+
+        def deal(dst, src, run):
+            nc.vector.tensor_copy(
+                dst.rearrange("p (t c i) -> p c t i", t=PACK, i=run),
+                src.rearrange("p (c i t) -> p c t i", t=PACK, i=run),
+            )
+
+        def interleave(copy, dst, src):
+            copy(dst[:].rearrange("p (c i) t -> p c t i", i=4), src[:].rearrange("p t (c i) -> p c t i", i=4))
+
+        def entries(tile, start, count):
+            return tile[:, start // PER_COL : (start + count) // PER_COL]
+
+        d_scale_table = sb("d_scale_table", [P, G], U8)
+        x_scale_table = sb("x_scale_table", [P, T], U8, tag="page0")
+        x_word_table = sb("x_word_table", [P, T], U32, tag="page1")
+        d_word_table = sb("d_word_table", [P, G], U32)
+
+        k1_l = load_list("k1_l", k1)
+        load_scale_rows(d_scale_table, d_scales)
+        offs_l = load_list("offs_l", offs)
+        load_scale_rows(x_scale_table, x_scales)
+        k2_l = load_list("k2_l", k2)
+        n1_l = load_list("n1_l", n1)
+        load_words(x_word_table, x_words)
+        load_words(d_word_table, d_words)
+        n2_l = load_list("n2_l", n2)
+        n4_l = load_list("n4_l", n4)
+        n3_l = load_list("n3_l", n3)
+
+        gs_t = sb("gs_t", [P, PACK], F32)
+        nc.gpsimd.dma_start(gs_t[:], gs.rearrange("(p t) o -> p (t o)", t=PACK))
+        gs_neg_half = sb("gs_neg_half", [P, PACK], F32)
+        nc.scalar.activation(gs_neg_half[:], gs_t[:], COPY, scale=-0.5)
+
+        placed1 = sb("placed1", [P, H + S], U8, tag="page3")
+        nc.vector.memset(placed1[:].bitcast(I32), 0)
+        placed2 = sb("placed2", [P, H], U8)
+        nc.vector.memset(placed2[:].bitcast(I32), 0)
+
+        picked_b1 = sb("picked_b1", [P, H + S], U8, tag="picked_b")
+        nc.vector.tensor_copy(picked_b1[:, :H], d_scale_table[:].indirect(k1_l[:]))
+        nc.vector.tensor_copy(picked_b1[:, H:], x_scale_table[:].indirect(offs_l[:]))
+        place_scale_rows(nc.scalar, placed1, picked_b1)
+        x_codes = sb("x_codes", [P, S], U32)
+        nc.vector.tensor_copy(x_codes[:], x_word_table[:].indirect(offs_l[:]))
+        picked_w1 = sb("picked_w1", [P, H], U32, tag="page2")
+        nc.vector.tensor_copy(picked_w1[:], d_word_table[:].indirect(k1_l[:]))
+        w1_codes = sb("w1_codes", [P, H], U32)
+        deal(w1_codes[:], picked_w1[:], 4)
+        w1_scales = sb("w1_scales", [P, H], U8)
+        deal(w1_scales[:], placed1[:, :H], 16)
+
+        picked_b2 = sb("picked_b2", [P, H], U8, tag="picked_b")
+        nc.vector.tensor_copy(picked_b2[:], d_scale_table[:].indirect(k2_l[:]))
+        place_scale_rows(nc.sync, placed2, picked_b2)
+
+        h = []
+        for t in range(PACK):
+            cols = slice(t * P, (t + 1) * P)
+            acc = psum.tile([P, 512], F32, name="acc", tag="acc")
+            nc.tensor.matmul_mx(
+                acc[:], lhsT=w1_codes[:, cols].bitcast(FP8X4), lhsT_scale=w1_scales[:, cols],
+                rhs=x_codes[:].bitcast(FP8X4), rhs_scale=placed1[:, H:], start=True, stop=True,
+            )
+            h_t = sb("h%d" % t, [P, S], F32)
+            nc.scalar.activation(h_t[:], acc[:], COPY, scale=0.0625)
+            h.append(h_t)
+
+        mem_rows = mem.rearrange("(p t) w -> t p w", t=PACK)
+        own, other = [], []
+        for t in range(PACK):
+            page = sb("page%d" % t, [P, U], F32)
+            nc.sync.dma_start(page[:], mem_rows[t])
+            nc.vector.tensor_copy(page[:].indirect(n1_l[:]), h[t][:])
+            other_t = sb("other%d" % t, [P, U], F32)
+            nc.scalar.activation(other_t[:], page[:], COPY, scale=gs_neg_half[:, t : t + 1])
+            own_t = sb("own%d" % t, [P, U], F32)
+            nc.scalar.activation(own_t[:], page[:], COPY, scale=gs_t[:, t : t + 1])
+            own.append(own_t)
+            other.append(other_t)
+
+        z_rounded = []
+        for c, (start, width) in enumerate(PIECES):
+            z = sb("z%d" % c, [P, PACK, width], F32)
+            for t in range(PACK):
+                nc.vector.tensor_tensor(
+                    z[:, t, :], other[t][:].indirect(entries(n2_l, start, width)), own[t][:, start : start + width], ADD
+                )
+            zb = sb("zb%d" % c, [P, width, PACK], BF16)
+            interleave(nc.scalar.copy, zb, z)
+            z_rounded.append(zb)
+
+        picked_w2 = sb("picked_w2", [P, H], U32, tag="own3")
+        nc.vector.tensor_copy(picked_w2[:], d_word_table[:].indirect(k2_l[:]))
+        w2_scales = sb("w2_scales", [P, H], U8)
+        deal(w2_scales[:], placed2[:], 16)
+        w2_codes = sb("w2_codes", [P, H], U32)
+        deal(w2_codes[:], picked_w2[:], 4)
+
+        z_codes, z_scales = [], []
+        for c, (start, width) in enumerate(PIECES):
+            codes = sb("z_codes%d" % c, [P, width], U32)
+            scales = sb("z_scales%d" % c, [P, width], U8)
+            nc.vector.quantize_mx(codes[:].bitcast(FP8X4), scales[:], z_rounded[c][:].rearrange("p w t -> p (w t)"))
+            z_codes.append(codes)
+            z_scales.append(scales)
+
+        h2 = []
+        for t in range(PACK):
+            cols = slice(t * P, (t + 1) * P)
+            h2_t = sb("h2_%d" % t, [P, U], F32)
+            for c, (start, width) in enumerate(PIECES):
+                acc = psum.tile([P, 512], F32, name="acc", tag="acc")
+                nc.tensor.matmul_mx(
+                    acc[:, :width], lhsT=w2_codes[:, cols].bitcast(FP8X4), lhsT_scale=w2_scales[:, cols],
+                    rhs=z_codes[c][:].bitcast(FP8X4), rhs_scale=z_scales[c][:], start=True, stop=True,
+                )
+                nc.scalar.activation(h2_t[:, start : start + width], acc[:, :width], COPY, scale=0.0625)
+            h2.append(h2_t)
+
+        out_rows = out_0.rearrange("(p t) w -> t p w", t=PACK)
+        out_words = out_1[0].rearrange("p c r -> p (c r)").bitcast(I32)
+        out_scales = sb("out_scales", [P, U], U8)
+        for c, (start, width) in enumerate(PIECES):
+            last = c == len(PIECES) - 1
+            y = sb("y%d" % c, [P, PACK, width], F32)
+            minus = sb("minus%d" % c, [P, PACK, width], F32)
+            for t in range(PACK + 1):
+                if t < PACK:
+                    nc.vector.tensor_copy(minus[:, t, :], h2[t][:].indirect(entries(n4_l, start, width)))
+                if t > 0:
+                    nc.vector.tensor_tensor(
+                        y[:, t - 1, :], h2[t - 1][:].indirect(entries(n3_l, start, width)), minus[:, t - 1, :], SUBTRACT
+                    )
+                    nc.sync.dma_start(out_rows[t - 1][:, start : start + width], y[:, t - 1, :])
+            yb = sb("yb%d" % c, [P, width, PACK], BF16)
+            interleave(nc.vector.tensor_copy if last else nc.scalar.copy, yb, y)
+            codes = sb("y_codes%d" % c, [P, width], U32)
+            nc.vector.quantize_mx(
+                codes[:].bitcast(FP8X4), out_scales[:, start : start + width], yb[:].rearrange("p w t -> p (w t)")
+            )
+            nc.sync.dma_start(out_words[:, start : start + width], codes[:].bitcast(I32))
+        for q in range(4):
+            queue = nc.scalar if q % 2 == 0 else nc.sync
+            queue.dma_start(
+                out_2[0][4 * q : 4 * q + 4, :].bitcast(I32), out_scales[32 * q : 32 * q + 4, :].bitcast(I32)
+            )

@@ -14,6 +14,7 @@ U8 = mybir.dt.uint8
 FP8X4 = mybir.dt.float8_e4m3fn_x4
 COPY = mybir.ActivationFunctionType.Copy
 ADD = mybir.AluOpType.add
+MULT = mybir.AluOpType.mult
 SUBTRACT = mybir.AluOpType.subtract
 
 P = 128
@@ -29,6 +30,9 @@ def tile_picked_codepagemgap_none_po_kernel(
     with ExitStack() as ctx:
         lists = ctx.enter_context(tc.tile_pool(name="lists", bufs=1))
         keep = ctx.enter_context(tc.tile_pool(name="keep", bufs=1))
+        paged = ctx.enter_context(tc.tile_pool(name="paged", bufs=1))
+        early = ctx.enter_context(tc.tile_pool(name="early", bufs=1))
+        late = ctx.enter_context(tc.tile_pool(name="late", bufs=1))
         psum = ctx.enter_context(tc.psum_pool(name="psum", bufs=8))
 
         def load_list(name, src):
@@ -43,38 +47,45 @@ def tile_picked_codepagemgap_none_po_kernel(
             rows = src[0].bitcast(I32)
             nc.sync.dma_start(tile[:].bitcast(I32), rows.unsqueeze(1).broadcast_to([16, 8, rows.shape[1]]))
 
-        def load_words(tile, src):
-            nc.sync.dma_start(tile[:].bitcast(I32), src[0].rearrange("p c r -> p (c r)").bitcast(I32))
+        def load_words(dst, src):
+            nc.sync.dma_start(dst.bitcast(I32), src[0].rearrange("p c r -> p (c r)").bitcast(I32))
 
         def place_scale_rows(queue, dst, src):
             for r in range(4):
                 queue.dma_start(dst[r:P:32, :].bitcast(I32), src[8 * r : P : 32, :].bitcast(I32))
 
-        def deal(dst, src, run):
+        def deal(dst, src, run, first, count):
             nc.vector.tensor_copy(
-                dst.rearrange("p (t c i) -> p c t i", t=PACK, i=run),
-                src.rearrange("p (c i t) -> p c t i", t=PACK, i=run),
+                dst.rearrange("p (t c i) -> p c t i", t=count, i=run),
+                src.rearrange("p (c i t) -> p c t i", t=PACK, i=run)[:, :, first : first + count, :],
             )
 
+        def at(pool, offset, name, shape, dtype):
+            return pool.tile(shape, dtype, name=name, align_bytes=64, offset=offset)
+
+        def columns(first, rest, t):
+            return first[:] if t == 0 else rest[:, (t - 1) * P : t * P]
+
         def interleave(copy, dst, src):
-            copy(dst[:].rearrange("p (c i) t -> p c t i", i=4), src[:].rearrange("p t (c i) -> p c t i", i=4))
+            copy(dst.rearrange("p (c i) t -> p c t i", i=4), src.rearrange("p t (c i) -> p c t i", i=4))
 
         def entries(tile, start, count):
             return tile[:, start // PER_COL : (start + count) // PER_COL]
 
         d_scale_table = sb("d_scale_table", [P, G], U8)
-        x_scale_table = sb("x_scale_table", [P, T], U8, tag="page0")
-        x_word_table = sb("x_word_table", [P, T], U32, tag="page1")
+        x_scale_table = sb("x_scale_table", [P, T], U8)
+        x_word_span = paged.tile([P, 2 * U + 512 + 16], U32, name="x_word_span", align_bytes=64, offset=2048)
+        x_word_table = x_word_span[:, :T]
         d_word_table = sb("d_word_table", [P, G], U32)
 
-        k1_l = load_list("k1_l", k1)
-        load_scale_rows(d_scale_table, d_scales)
         offs_l = load_list("offs_l", offs)
         load_scale_rows(x_scale_table, x_scales)
+        k1_l = load_list("k1_l", k1)
+        load_scale_rows(d_scale_table, d_scales)
         k2_l = load_list("k2_l", k2)
         n1_l = load_list("n1_l", n1)
         load_words(x_word_table, x_words)
-        load_words(d_word_table, d_words)
+        load_words(d_word_table[:], d_words)
         n2_l = load_list("n2_l", n2)
         n4_l = load_list("n4_l", n4)
         n3_l = load_list("n3_l", n3)
@@ -82,36 +93,39 @@ def tile_picked_codepagemgap_none_po_kernel(
         gs_t = sb("gs_t", [P, PACK], F32)
         nc.gpsimd.dma_start(gs_t[:], gs.rearrange("(p t) o -> p (t o)", t=PACK))
         gs_neg_half = sb("gs_neg_half", [P, PACK], F32)
-        nc.scalar.activation(gs_neg_half[:], gs_t[:], COPY, scale=-0.5)
+        nc.gpsimd.tensor_scalar(gs_neg_half[:], gs_t[:], -0.5, 0.0, MULT, ADD)
 
-        placed1 = sb("placed1", [P, H + S], U8, tag="page3")
+        placed1 = sb("placed1", [P, H + S], U8)
         nc.vector.memset(placed1[:].bitcast(I32), 0)
         placed2 = sb("placed2", [P, H], U8)
         nc.vector.memset(placed2[:].bitcast(I32), 0)
 
-        picked_b1 = sb("picked_b1", [P, H + S], U8, tag="picked_b")
-        nc.vector.tensor_copy(picked_b1[:, :H], d_scale_table[:].indirect(k1_l[:]))
+        picked_b1 = at(early, 0, "picked_b1", [P, H + S], U8)
         nc.vector.tensor_copy(picked_b1[:, H:], x_scale_table[:].indirect(offs_l[:]))
+        nc.vector.tensor_copy(picked_b1[:, :H], d_scale_table[:].indirect(k1_l[:]))
         place_scale_rows(nc.scalar, placed1, picked_b1)
         x_codes = sb("x_codes", [P, S], U32)
-        nc.vector.tensor_copy(x_codes[:], x_word_table[:].indirect(offs_l[:]))
-        picked_w1 = sb("picked_w1", [P, H], U32, tag="page2")
+        nc.vector.tensor_copy(x_codes[:], x_word_table.indirect(offs_l[:]))
+        picked_w1 = sb("picked_w1", [P, H], U32)
         nc.vector.tensor_copy(picked_w1[:], d_word_table[:].indirect(k1_l[:]))
-        w1_codes = sb("w1_codes", [P, H], U32)
-        deal(w1_codes[:], picked_w1[:], 4)
-        w1_scales = sb("w1_scales", [P, H], U8)
-        deal(w1_scales[:], placed1[:, :H], 16)
+        w1_codes0 = sb("w1_codes0", [P, P], U32)
+        deal(w1_codes0[:], picked_w1[:], 4, 0, 1)
+        w1_scales0 = sb("w1_scales0", [P, P], U8)
+        deal(w1_scales0[:], placed1[:, :H], 16, 0, 1)
+        w1_codes = at(early, H, "w1_codes", [P, 3 * P], U32)
+        deal(w1_codes[:], picked_w1[:], 4, 1, 3)
+        w1_scales = sb("w1_scales", [P, 3 * P], U8)
+        deal(w1_scales[:], placed1[:, :H], 16, 1, 3)
 
-        picked_b2 = sb("picked_b2", [P, H], U8, tag="picked_b")
+        picked_b2 = at(early, 0, "picked_b2", [P, H], U8)
         nc.vector.tensor_copy(picked_b2[:], d_scale_table[:].indirect(k2_l[:]))
         place_scale_rows(nc.sync, placed2, picked_b2)
 
         h = []
         for t in range(PACK):
-            cols = slice(t * P, (t + 1) * P)
             acc = psum.tile([P, 512], F32, name="acc", tag="acc")
             nc.tensor.matmul_mx(
-                acc[:], lhsT=w1_codes[:, cols].bitcast(FP8X4), lhsT_scale=w1_scales[:, cols],
+                acc[:], lhsT=columns(w1_codes0, w1_codes, t).bitcast(FP8X4), lhsT_scale=columns(w1_scales0, w1_scales, t),
                 rhs=x_codes[:].bitcast(FP8X4), rhs_scale=placed1[:, H:], start=True, stop=True,
             )
             h_t = sb("h%d" % t, [P, S], F32)
@@ -121,33 +135,40 @@ def tile_picked_codepagemgap_none_po_kernel(
         mem_rows = mem.rearrange("(p t) w -> t p w", t=PACK)
         own, other = [], []
         for t in range(PACK):
-            page = sb("page%d" % t, [P, U], F32)
+            page = paged.tile([P, U], F32, name="page%d" % t, align_bytes=64, offset=4096 * t)
             nc.sync.dma_start(page[:], mem_rows[t])
             nc.vector.tensor_copy(page[:].indirect(n1_l[:]), h[t][:])
             other_t = sb("other%d" % t, [P, U], F32)
             nc.scalar.activation(other_t[:], page[:], COPY, scale=gs_neg_half[:, t : t + 1])
-            own_t = sb("own%d" % t, [P, U], F32)
-            nc.scalar.activation(own_t[:], page[:], COPY, scale=gs_t[:, t : t + 1])
-            own.append(own_t)
+            halves = []
+            for u in range(2):
+                if (t, u) == (3, 0):
+                    own_tu = at(late, 0, "own3_0", [P, 512], F32)
+                else:
+                    own_tu = sb("own%d_%d" % (t, u), [P, 512], F32)
+                nc.scalar.activation(own_tu[:], page[:, 512 * u : 512 * (u + 1)], COPY, scale=gs_t[:, t : t + 1])
+                halves.append(own_tu)
+            own.append(halves)
             other.append(other_t)
 
         z_rounded = []
+        z_first = sb("z_first", [P, PACK, 512], F32, tag="h3")
+        z_rest = at(late, 0, "z_rest", [P, 2 * PACK, 256], F32)
         for c, (start, width) in enumerate(PIECES):
-            z = sb("z%d" % c, [P, PACK, width], F32)
+            z = z_first[:] if c == 0 else z_rest[:, PACK * (c - 1) : PACK * c, :]
             for t in range(PACK):
-                nc.vector.tensor_tensor(
-                    z[:, t, :], other[t][:].indirect(entries(n2_l, start, width)), own[t][:, start : start + width], ADD
-                )
+                mine = own[t][start // 512][:, start % 512 : start % 512 + width]
+                nc.vector.tensor_tensor(z[:, t, :], other[t][:].indirect(entries(n2_l, start, width)), mine, ADD)
             zb = sb("zb%d" % c, [P, width, PACK], BF16)
-            interleave(nc.scalar.copy, zb, z)
+            interleave(nc.scalar.copy, zb[:], z)
             z_rounded.append(zb)
 
-        picked_w2 = sb("picked_w2", [P, H], U32, tag="own3")
+        picked_w2 = sb("picked_w2", [P, H], U32, tag="own2_1")
         nc.vector.tensor_copy(picked_w2[:], d_word_table[:].indirect(k2_l[:]))
-        w2_scales = sb("w2_scales", [P, H], U8)
-        deal(w2_scales[:], placed2[:], 16)
-        w2_codes = sb("w2_codes", [P, H], U32)
-        deal(w2_codes[:], picked_w2[:], 4)
+        w2_scales0 = sb("w2_scales0", [P, P], U8, tag="own1_1")
+        deal(w2_scales0[:], placed2[:], 16, 0, 1)
+        w2_codes0 = sb("w2_codes0", [P, P], U32)
+        deal(w2_codes0[:], picked_w2[:], 4, 0, 1)
 
         z_codes, z_scales = [], []
         for c, (start, width) in enumerate(PIECES):
@@ -156,42 +177,67 @@ def tile_picked_codepagemgap_none_po_kernel(
             nc.vector.quantize_mx(codes[:].bitcast(FP8X4), scales[:], z_rounded[c][:].rearrange("p w t -> p (w t)"))
             z_codes.append(codes)
             z_scales.append(scales)
+        w2_codes = at(late, 0, "w2_codes", [P, 3 * P], U32)
+        deal(w2_codes[:], picked_w2[:], 4, 1, 3)
+        w2_scales = at(late, 2048, "w2_scales", [P, 3 * P], U8)
+        deal(w2_scales[:], placed2[:], 16, 1, 3)
 
         h2 = []
         for t in range(PACK):
-            cols = slice(t * P, (t + 1) * P)
             h2_t = sb("h2_%d" % t, [P, U], F32)
             for c, (start, width) in enumerate(PIECES):
                 acc = psum.tile([P, 512], F32, name="acc", tag="acc")
                 nc.tensor.matmul_mx(
-                    acc[:, :width], lhsT=w2_codes[:, cols].bitcast(FP8X4), lhsT_scale=w2_scales[:, cols],
+                    acc[:, :width], lhsT=columns(w2_codes0, w2_codes, t).bitcast(FP8X4), lhsT_scale=columns(w2_scales0, w2_scales, t),
                     rhs=z_codes[c][:].bitcast(FP8X4), rhs_scale=z_scales[c][:], start=True, stop=True,
                 )
-                nc.scalar.activation(h2_t[:, start : start + width], acc[:, :width], COPY, scale=0.0625)
+                if (t, c) == (0, 2):
+                    nc.vector.tensor_scalar_mul(h2_t[:, start : start + width], acc[:, :width], 0.0625)
+                else:
+                    nc.scalar.activation(h2_t[:, start : start + width], acc[:, :width], COPY, scale=0.0625)
             h2.append(h2_t)
 
         out_rows = out_0.rearrange("(p t) w -> t p w", t=PACK)
         out_words = out_1[0].rearrange("p c r -> p (c r)").bitcast(I32)
         out_scales = sb("out_scales", [P, U], U8)
-        for c, (start, width) in enumerate(PIECES):
-            last = c == len(PIECES) - 1
-            y = sb("y%d" % c, [P, PACK, width], F32)
-            minus = sb("minus%d" % c, [P, PACK, width], F32)
-            for t in range(PACK + 1):
-                if t < PACK:
-                    nc.vector.tensor_copy(minus[:, t, :], h2[t][:].indirect(entries(n4_l, start, width)))
-                if t > 0:
-                    nc.vector.tensor_tensor(
-                        y[:, t - 1, :], h2[t - 1][:].indirect(entries(n3_l, start, width)), minus[:, t - 1, :], SUBTRACT
-                    )
-                    nc.sync.dma_start(out_rows[t - 1][:, start : start + width], y[:, t - 1, :])
+        def fetch_minus(dst, t, c):
+            nc.vector.tensor_copy(dst, h2[t][:].indirect(entries(n4_l, *PIECES[c])))
+
+        def fetch_difference(dst, minus, t, c):
+            start, width = PIECES[c]
+            nc.vector.tensor_tensor(dst, h2[t][:].indirect(entries(n3_l, start, width)), minus, SUBTRACT)
+            nc.sync.dma_start(out_rows[t][:, start : start + width], dst)
+
+        def hand_on(c, y):
+            start, width = PIECES[c]
             yb = sb("yb%d" % c, [P, width, PACK], BF16)
-            interleave(nc.vector.tensor_copy if last else nc.scalar.copy, yb, y)
+            if c == len(PIECES) - 1:
+                interleave(nc.vector.tensor_copy, yb[:, :80, :], y[:, :, :80])
+                interleave(nc.scalar.copy, yb[:, 80:, :], y[:, :, 80:])
+            else:
+                interleave(nc.scalar.copy, yb[:], y[:])
             codes = sb("y_codes%d" % c, [P, width], U32)
             nc.vector.quantize_mx(
                 codes[:].bitcast(FP8X4), out_scales[:, start : start + width], yb[:].rearrange("p w t -> p (w t)")
             )
             nc.sync.dma_start(out_words[:, start : start + width], codes[:].bitcast(I32))
+
+        y = [sb("y%d" % c, [P, PACK, width], F32) for c, (start, width) in enumerate(PIECES)]
+        minus = [sb("minus%d" % c, [P, PACK, width], F32, tag="minus%d" % (c % 2)) for c, (start, width) in enumerate(PIECES[:2])]
+        for t in range(PACK):
+            for c in (0, 1):
+                fetch_minus(minus[c][:, t, :], t, c)
+            for c in (0, 1):
+                fetch_difference(y[c][:, t, :], minus[c][:, t, :], t, c)
+        hand_on(0, y[0])
+        hand_on(1, y[1])
+        minus_last = sb("minus_last", [P, PACK, 256], F32, tag="minus0")
+        for t in range(PACK + 1):
+            if t < PACK:
+                fetch_minus(minus_last[:, t, :], t, 2)
+            if t > 0:
+                fetch_difference(y[2][:, t - 1, :], minus_last[:, t - 1, :], t - 1, 2)
+        hand_on(2, y[2])
         for q in range(4):
             queue = nc.scalar if q % 2 == 0 else nc.sync
             queue.dma_start(

@@ -32,7 +32,6 @@ def tile_picked_codepagemgap_none_po_kernel(
         keep = ctx.enter_context(tc.tile_pool(name="keep", bufs=1))
         paged = ctx.enter_context(tc.tile_pool(name="paged", bufs=1))
         early = ctx.enter_context(tc.tile_pool(name="early", bufs=1))
-        late = ctx.enter_context(tc.tile_pool(name="late", bufs=1))
         psum = ctx.enter_context(tc.psum_pool(name="psum", bufs=8))
 
         def load_list(name, src):
@@ -142,18 +141,15 @@ def tile_picked_codepagemgap_none_po_kernel(
             nc.scalar.activation(other_t[:], page[:], COPY, scale=gs_neg_half[:, t : t + 1])
             halves = []
             for u in range(2):
-                if (t, u) == (3, 0):
-                    own_tu = at(late, 0, "own3_0", [P, 512], F32)
-                else:
-                    own_tu = sb("own%d_%d" % (t, u), [P, 512], F32)
+                own_tu = sb("own%d_%d" % (t, u), [P, 512], F32)
                 nc.scalar.activation(own_tu[:], page[:, 512 * u : 512 * (u + 1)], COPY, scale=gs_t[:, t : t + 1])
                 halves.append(own_tu)
             own.append(halves)
             other.append(other_t)
 
         z_rounded = []
-        z_first = sb("z_first", [P, PACK, 512], F32, tag="h3")
-        z_rest = at(late, 0, "z_rest", [P, 2 * PACK, 256], F32)
+        z_first = at(paged, 4096, "z_first", [P, PACK, 512], F32)
+        z_rest = at(paged, 3 * 4096, "z_rest", [P, 2 * PACK, 256], F32)
         for c, (start, width) in enumerate(PIECES):
             z = z_first[:] if c == 0 else z_rest[:, PACK * (c - 1) : PACK * c, :]
             for t in range(PACK):
@@ -177,9 +173,9 @@ def tile_picked_codepagemgap_none_po_kernel(
             nc.vector.quantize_mx(codes[:].bitcast(FP8X4), scales[:], z_rounded[c][:].rearrange("p w t -> p (w t)"))
             z_codes.append(codes)
             z_scales.append(scales)
-        w2_codes = at(late, 0, "w2_codes", [P, 3 * P], U32)
+        w2_codes = at(paged, 4 * 4096, "w2_codes", [P, 3 * P], U32)
         deal(w2_codes[:], picked_w2[:], 4, 1, 3)
-        w2_scales = at(late, 2048, "w2_scales", [P, 3 * P], U8)
+        w2_scales = at(paged, 4 * 4096 + 2048, "w2_scales", [P, 3 * P], U8)
         deal(w2_scales[:], placed2[:], 16, 1, 3)
 
         h2 = []

@@ -19,8 +19,17 @@ SUBTRACT = mybir.AluOpType.subtract
 
 P = 128
 PACK = 4
-PER_COL = 16
+SCALE_ROWS = 16
+QUADRANT = 32
+ENTRIES_PER_COLUMN = 16
+BANK = 512
+PSUM_BANKS = 8
+LINE = 16
+PAGE_BYTES = 4 * U
+SIXTEENTH = 0.0625
+
 PIECES = [(0, 512), (512, 256), (768, 256)]
+LAST_ON_VECTOR = 80
 
 
 def tile_picked_codepagemgap_none_po_kernel(
@@ -32,50 +41,66 @@ def tile_picked_codepagemgap_none_po_kernel(
         keep = ctx.enter_context(tc.tile_pool(name="keep", bufs=1))
         paged = ctx.enter_context(tc.tile_pool(name="paged", bufs=1))
         early = ctx.enter_context(tc.tile_pool(name="early", bufs=1))
-        psum = ctx.enter_context(tc.psum_pool(name="psum", bufs=8))
+        psum = ctx.enter_context(tc.psum_pool(name="psum", bufs=PSUM_BANKS))
+
+        def kept(name, shape, dtype, tag=None):
+            return keep.tile(shape, dtype, name=name, tag=tag or name, align_bytes=64)
+
+        def placed_at(pool, offset, name, shape, dtype):
+            return pool.tile(shape, dtype, name=name, align_bytes=64, offset=offset)
 
         def load_list(name, src):
             tile = lists.tile(list(src.shape), U16, name=name)
             nc.sync.dma_start(tile[:], src)
             return tile
 
-        def sb(name, shape, dtype, tag=None):
-            return keep.tile(shape, dtype, name=name, tag=tag or name, align_bytes=64)
+        def entries(tile, start, count):
+            return tile[:, start // ENTRIES_PER_COLUMN : (start + count) // ENTRIES_PER_COLUMN]
 
         def load_scale_rows(tile, src):
             rows = src[0].bitcast(I32)
-            nc.sync.dma_start(tile[:].bitcast(I32), rows.unsqueeze(1).broadcast_to([16, 8, rows.shape[1]]))
+            spread = rows.unsqueeze(1).broadcast_to([SCALE_ROWS, P // SCALE_ROWS, rows.shape[1]])
+            nc.sync.dma_start(tile[:].bitcast(I32), spread)
 
         def load_words(dst, src):
             nc.sync.dma_start(dst.bitcast(I32), src[0].rearrange("p c r -> p (c r)").bitcast(I32))
 
-        def place_scale_rows(queue, dst, src):
+        def move_scale_rows(queues, dst, src):
             for r in range(4):
-                queue.dma_start(dst[r:P:32, :].bitcast(I32), src[8 * r : P : 32, :].bitcast(I32))
+                queues[r % len(queues)].dma_start(
+                    dst[r:P:QUADRANT, :].bitcast(I32), src[8 * r : P : QUADRANT, :].bitcast(I32)
+                )
 
-        def deal(dst, src, run, first, count):
+        def deal(dst, src, per_line, first, count):
             nc.vector.tensor_copy(
-                dst.rearrange("p (t c i) -> p c t i", t=count, i=run),
-                src.rearrange("p (c i t) -> p c t i", t=PACK, i=run)[:, :, first : first + count, :],
+                dst.rearrange("p (t c i) -> p c t i", t=count, i=per_line),
+                src.rearrange("p (c i t) -> p c t i", t=PACK, i=per_line)[:, :, first : first + count, :],
             )
 
-        def at(pool, offset, name, shape, dtype):
-            return pool.tile(shape, dtype, name=name, align_bytes=64, offset=offset)
-
-        def columns(first, rest, t):
-            return first[:] if t == 0 else rest[:, (t - 1) * P : t * P]
+        def plane_columns(plane_0, planes_1_to_3, t):
+            return plane_0[:] if t == 0 else planes_1_to_3[:, (t - 1) * P : t * P]
 
         def interleave(copy, dst, src):
             copy(dst.rearrange("p (c i) t -> p c t i", i=4), src.rearrange("p t (c i) -> p c t i", i=4))
 
-        def entries(tile, start, count):
-            return tile[:, start // PER_COL : (start + count) // PER_COL]
+        def product(width, codes, scales, moving_codes, moving_scales):
+            acc = psum.tile([P, BANK], F32, name="acc", tag="acc")
+            nc.tensor.matmul_mx(
+                acc[:, :width],
+                lhsT=codes.bitcast(FP8X4),
+                lhsT_scale=scales,
+                rhs=moving_codes.bitcast(FP8X4),
+                rhs_scale=moving_scales,
+                start=True,
+                stop=True,
+            )
+            return acc[:, :width]
 
-        d_scale_table = sb("d_scale_table", [P, G], U8)
-        x_scale_table = sb("x_scale_table", [P, T], U8)
-        x_word_span = paged.tile([P, 2 * U + 512 + 16], U32, name="x_word_span", align_bytes=64, offset=2048)
+        d_scale_table = kept("d_scale_table", [P, G], U8)
+        x_scale_table = kept("x_scale_table", [P, T], U8)
+        x_word_span = placed_at(paged, PAGE_BYTES // 2, "x_word_span", [P, 2 * U + U // 2 + LINE], U32)
         x_word_table = x_word_span[:, :T]
-        d_word_table = sb("d_word_table", [P, G], U32)
+        d_word_table = kept("d_word_table", [P, G], U32)
 
         offs_l = load_list("offs_l", offs)
         load_scale_rows(x_scale_table, x_scales)
@@ -89,153 +114,164 @@ def tile_picked_codepagemgap_none_po_kernel(
         n4_l = load_list("n4_l", n4)
         n3_l = load_list("n3_l", n3)
 
-        gs_t = sb("gs_t", [P, PACK], F32)
+        gs_t = kept("gs_t", [P, PACK], F32)
         nc.gpsimd.dma_start(gs_t[:], gs.rearrange("(p t) o -> p (t o)", t=PACK))
-        gs_neg_half = sb("gs_neg_half", [P, PACK], F32)
+        gs_neg_half = kept("gs_neg_half", [P, PACK], F32)
         nc.gpsimd.tensor_scalar(gs_neg_half[:], gs_t[:], -0.5, 0.0, MULT, ADD)
 
-        placed1 = sb("placed1", [P, H + S], U8)
-        nc.vector.memset(placed1[:].bitcast(I32), 0)
-        placed2 = sb("placed2", [P, H], U8)
-        nc.vector.memset(placed2[:].bitcast(I32), 0)
+        moved_b1 = kept("moved_b1", [P, H + S], U8)
+        nc.vector.memset(moved_b1[:].bitcast(I32), 0)
+        moved_b2 = kept("moved_b2", [P, H], U8)
+        nc.vector.memset(moved_b2[:].bitcast(I32), 0)
 
-        picked_b1 = at(early, 0, "picked_b1", [P, H + S], U8)
+        picked_b1 = placed_at(early, 0, "picked_b1", [P, H + S], U8)
         nc.vector.tensor_copy(picked_b1[:, H:], x_scale_table[:].indirect(offs_l[:]))
         nc.vector.tensor_copy(picked_b1[:, :H], d_scale_table[:].indirect(k1_l[:]))
-        place_scale_rows(nc.scalar, placed1, picked_b1)
-        x_codes = sb("x_codes", [P, S], U32)
+        move_scale_rows([nc.scalar, nc.sync], moved_b1, picked_b1)
+        x_codes = kept("x_codes", [P, S], U32)
         nc.vector.tensor_copy(x_codes[:], x_word_table.indirect(offs_l[:]))
-        picked_w1 = sb("picked_w1", [P, H], U32)
+        picked_w1 = kept("picked_w1", [P, H], U32)
         nc.vector.tensor_copy(picked_w1[:], d_word_table[:].indirect(k1_l[:]))
-        w1_codes0 = sb("w1_codes0", [P, P], U32)
-        deal(w1_codes0[:], picked_w1[:], 4, 0, 1)
-        w1_scales0 = sb("w1_scales0", [P, P], U8)
-        deal(w1_scales0[:], placed1[:, :H], 16, 0, 1)
-        w1_codes = at(early, H, "w1_codes", [P, 3 * P], U32)
-        deal(w1_codes[:], picked_w1[:], 4, 1, 3)
-        w1_scales = sb("w1_scales", [P, 3 * P], U8)
-        deal(w1_scales[:], placed1[:, :H], 16, 1, 3)
+        w1_scales_0 = kept("w1_scales_0", [P, P], U8)
+        deal(w1_scales_0[:], moved_b1[:, :H], LINE, 0, 1)
+        w1_codes = placed_at(early, H, "w1_codes", [P, H], U32)
+        deal(w1_codes[:, :P], picked_w1[:], LINE // 4, 0, 1)
+        deal(w1_codes[:, P:], picked_w1[:], LINE // 4, 1, PACK - 1)
+        w1_scales_rest = kept("w1_scales_rest", [P, (PACK - 1) * P], U8)
+        deal(w1_scales_rest[:], moved_b1[:, :H], LINE, 1, PACK - 1)
 
-        picked_b2 = at(early, 0, "picked_b2", [P, H], U8)
+        picked_b2 = placed_at(early, 0, "picked_b2", [P, H], U8)
         nc.vector.tensor_copy(picked_b2[:], d_scale_table[:].indirect(k2_l[:]))
-        place_scale_rows(nc.sync, placed2, picked_b2)
+        move_scale_rows([nc.sync], moved_b2, picked_b2)
 
         h = []
         for t in range(PACK):
-            acc = psum.tile([P, 512], F32, name="acc", tag="acc")
-            nc.tensor.matmul_mx(
-                acc[:], lhsT=columns(w1_codes0, w1_codes, t).bitcast(FP8X4), lhsT_scale=columns(w1_scales0, w1_scales, t),
-                rhs=x_codes[:].bitcast(FP8X4), rhs_scale=placed1[:, H:], start=True, stop=True,
-            )
-            h_t = sb("h%d" % t, [P, S], F32)
-            nc.scalar.activation(h_t[:], acc[:], COPY, scale=0.0625)
+            h_t = kept("h%d" % t, [P, S], F32)
+            width = S // 2 if t == 0 else S
+            for start in range(0, S, width):
+                acc = product(
+                    width,
+                    w1_codes[:, t * P : (t + 1) * P],
+                    plane_columns(w1_scales_0, w1_scales_rest, t),
+                    x_codes[:, start : start + width],
+                    moved_b1[:, H + start : H + start + width],
+                )
+                nc.scalar.activation(h_t[:, start : start + width], acc, COPY, scale=SIXTEENTH)
             h.append(h_t)
 
-        mem_rows = mem.rearrange("(p t) w -> t p w", t=PACK)
+        mem_planes = mem.rearrange("(p t) w -> t p w", t=PACK)
+        half = U // 2
         own, other = [], []
         for t in range(PACK):
-            page = paged.tile([P, U], F32, name="page%d" % t, align_bytes=64, offset=4096 * t)
-            nc.sync.dma_start(page[:], mem_rows[t])
+            page = placed_at(paged, t * PAGE_BYTES, "page%d" % t, [P, U], F32)
+            nc.sync.dma_start(page[:], mem_planes[t])
             nc.vector.tensor_copy(page[:].indirect(n1_l[:]), h[t][:])
-            other_t = sb("other%d" % t, [P, U], F32)
+            other_t = kept("other%d" % t, [P, U], F32)
             nc.scalar.activation(other_t[:], page[:], COPY, scale=gs_neg_half[:, t : t + 1])
             halves = []
             for u in range(2):
-                own_tu = sb("own%d_%d" % (t, u), [P, 512], F32)
-                nc.scalar.activation(own_tu[:], page[:, 512 * u : 512 * (u + 1)], COPY, scale=gs_t[:, t : t + 1])
+                own_tu = kept("own%d_%d" % (t, u), [P, half], F32)
+                nc.scalar.activation(own_tu[:], page[:, half * u : half * (u + 1)], COPY, scale=gs_t[:, t : t + 1])
                 halves.append(own_tu)
             own.append(halves)
             other.append(other_t)
 
+        z_first = placed_at(paged, PAGE_BYTES, "z_first", [P, PACK, PIECES[0][1]], F32)
+        z_rest = placed_at(paged, 3 * PAGE_BYTES, "z_rest", [P, 2 * PACK, PIECES[1][1]], F32)
         z_rounded = []
-        z_first = at(paged, 4096, "z_first", [P, PACK, 512], F32)
-        z_rest = at(paged, 3 * 4096, "z_rest", [P, 2 * PACK, 256], F32)
         for c, (start, width) in enumerate(PIECES):
             z = z_first[:] if c == 0 else z_rest[:, PACK * (c - 1) : PACK * c, :]
             for t in range(PACK):
-                mine = own[t][start // 512][:, start % 512 : start % 512 + width]
-                nc.vector.tensor_tensor(z[:, t, :], other[t][:].indirect(entries(n2_l, start, width)), mine, ADD)
-            zb = sb("zb%d" % c, [P, width, PACK], BF16)
-            interleave(nc.scalar.copy, zb[:], z)
-            z_rounded.append(zb)
+                own_piece = own[t][start // half][:, start % half : start % half + width]
+                nc.vector.tensor_tensor(z[:, t, :], other[t][:].indirect(entries(n2_l, start, width)), own_piece, ADD)
+            z_bf16 = kept("z_bf16_%d" % c, [P, width, PACK], BF16)
+            interleave(nc.scalar.copy, z_bf16[:], z)
+            z_rounded.append(z_bf16)
 
-        picked_w2 = sb("picked_w2", [P, H], U32, tag="own2_1")
+        picked_w2 = kept("picked_w2", [P, H], U32, tag="own2_1")
         nc.vector.tensor_copy(picked_w2[:], d_word_table[:].indirect(k2_l[:]))
-        w2_scales0 = sb("w2_scales0", [P, P], U8, tag="own1_1")
-        deal(w2_scales0[:], placed2[:], 16, 0, 1)
-        w2_codes0 = sb("w2_codes0", [P, P], U32)
-        deal(w2_codes0[:], picked_w2[:], 4, 0, 1)
 
         z_codes, z_scales = [], []
         for c, (start, width) in enumerate(PIECES):
-            codes = sb("z_codes%d" % c, [P, width], U32)
-            scales = sb("z_scales%d" % c, [P, width], U8)
+            codes = kept("z_codes%d" % c, [P, width], U32)
+            scales = kept("z_scales%d" % c, [P, width], U8)
             nc.vector.quantize_mx(codes[:].bitcast(FP8X4), scales[:], z_rounded[c][:].rearrange("p w t -> p (w t)"))
             z_codes.append(codes)
             z_scales.append(scales)
-        w2_codes = at(paged, 4 * 4096, "w2_codes", [P, 3 * P], U32)
-        deal(w2_codes[:], picked_w2[:], 4, 1, 3)
-        w2_scales = at(paged, 4 * 4096 + 2048, "w2_scales", [P, 3 * P], U8)
-        deal(w2_scales[:], placed2[:], 16, 1, 3)
+            if c == 0:
+                w2_scales_0 = kept("w2_scales_0", [P, P], U8, tag="own1_1")
+                deal(w2_scales_0[:], moved_b2[:], LINE, 0, 1)
+                w2_codes_0 = kept("w2_codes_0", [P, P], U32)
+                deal(w2_codes_0[:], picked_w2[:], LINE // 4, 0, 1)
+        w2_codes_rest = placed_at(paged, 4 * PAGE_BYTES, "w2_codes_rest", [P, (PACK - 1) * P], U32)
+        deal(w2_codes_rest[:], picked_w2[:], LINE // 4, 1, PACK - 1)
+        w2_scales_rest = placed_at(paged, 4 * PAGE_BYTES + PAGE_BYTES // 2, "w2_scales_rest", [P, (PACK - 1) * P], U8)
+        deal(w2_scales_rest[:], moved_b2[:], LINE, 1, PACK - 1)
 
+        last_piece = len(PIECES) - 1
         h2 = []
         for t in range(PACK):
-            h2_t = sb("h2_%d" % t, [P, U], F32)
+            h2_t = kept("h2_%d" % t, [P, U], F32)
             for c, (start, width) in enumerate(PIECES):
-                acc = psum.tile([P, 512], F32, name="acc", tag="acc")
-                nc.tensor.matmul_mx(
-                    acc[:, :width], lhsT=columns(w2_codes0, w2_codes, t).bitcast(FP8X4), lhsT_scale=columns(w2_scales0, w2_scales, t),
-                    rhs=z_codes[c][:].bitcast(FP8X4), rhs_scale=z_scales[c][:], start=True, stop=True,
+                acc = product(
+                    width,
+                    plane_columns(w2_codes_0, w2_codes_rest, t),
+                    plane_columns(w2_scales_0, w2_scales_rest, t),
+                    z_codes[c][:],
+                    z_scales[c][:],
                 )
-                if (t, c) == (0, 2):
-                    nc.vector.tensor_scalar_mul(h2_t[:, start : start + width], acc[:, :width], 0.0625)
+                if t == 0 and c == last_piece:
+                    nc.vector.tensor_scalar_mul(h2_t[:, start : start + width], acc, SIXTEENTH)
                 else:
-                    nc.scalar.activation(h2_t[:, start : start + width], acc[:, :width], COPY, scale=0.0625)
+                    nc.scalar.activation(h2_t[:, start : start + width], acc, COPY, scale=SIXTEENTH)
             h2.append(h2_t)
 
-        out_rows = out_0.rearrange("(p t) w -> t p w", t=PACK)
+        out_planes = out_0.rearrange("(p t) w -> t p w", t=PACK)
         out_words = out_1[0].rearrange("p c r -> p (c r)").bitcast(I32)
-        out_scales = sb("out_scales", [P, U], U8)
-        def fetch_minus(dst, t, c):
+        out_scales = kept("out_scales", [P, U], U8)
+
+        def fetch_subtrahend(dst, t, c):
             nc.vector.tensor_copy(dst, h2[t][:].indirect(entries(n4_l, *PIECES[c])))
 
-        def fetch_difference(dst, minus, t, c):
+        def fetch_difference(dst, subtrahend, t, c):
             start, width = PIECES[c]
-            nc.vector.tensor_tensor(dst, h2[t][:].indirect(entries(n3_l, start, width)), minus, SUBTRACT)
-            nc.sync.dma_start(out_rows[t][:, start : start + width], dst)
+            nc.vector.tensor_tensor(dst, h2[t][:].indirect(entries(n3_l, start, width)), subtrahend, SUBTRACT)
+            nc.sync.dma_start(out_planes[t][:, start : start + width], dst)
 
-        def hand_on(c, y):
+        def quantise_piece(c, y_piece):
             start, width = PIECES[c]
-            yb = sb("yb%d" % c, [P, width, PACK], BF16)
-            if c == len(PIECES) - 1:
-                interleave(nc.vector.tensor_copy, yb[:, :80, :], y[:, :, :80])
-                interleave(nc.scalar.copy, yb[:, 80:, :], y[:, :, 80:])
+            y_bf16 = kept("y_bf16_%d" % c, [P, width, PACK], BF16)
+            if c == last_piece:
+                interleave(nc.vector.tensor_copy, y_bf16[:, :LAST_ON_VECTOR, :], y_piece[:, :, :LAST_ON_VECTOR])
+                interleave(nc.scalar.copy, y_bf16[:, LAST_ON_VECTOR:, :], y_piece[:, :, LAST_ON_VECTOR:])
             else:
-                interleave(nc.scalar.copy, yb[:], y[:])
-            codes = sb("y_codes%d" % c, [P, width], U32)
+                interleave(nc.scalar.copy, y_bf16[:], y_piece[:])
+            codes = kept("y_codes%d" % c, [P, width], U32)
             nc.vector.quantize_mx(
-                codes[:].bitcast(FP8X4), out_scales[:, start : start + width], yb[:].rearrange("p w t -> p (w t)")
+                codes[:].bitcast(FP8X4), out_scales[:, start : start + width], y_bf16[:].rearrange("p w t -> p (w t)")
             )
             nc.sync.dma_start(out_words[:, start : start + width], codes[:].bitcast(I32))
 
-        y = [sb("y%d" % c, [P, PACK, width], F32) for c, (start, width) in enumerate(PIECES)]
-        minus = [sb("minus%d" % c, [P, PACK, width], F32, tag="minus%d" % (c % 2)) for c, (start, width) in enumerate(PIECES[:2])]
+        y = [kept("y%d" % c, [P, PACK, width], F32) for c, (start, width) in enumerate(PIECES)]
+        minus = [kept("minus%d" % c, [P, PACK, width], F32) for c, (start, width) in enumerate(PIECES[:last_piece])]
         for t in range(PACK):
-            for c in (0, 1):
-                fetch_minus(minus[c][:, t, :], t, c)
-            for c in (0, 1):
+            for c in range(last_piece):
+                fetch_subtrahend(minus[c][:, t, :], t, c)
+            for c in range(last_piece):
                 fetch_difference(y[c][:, t, :], minus[c][:, t, :], t, c)
-        hand_on(0, y[0])
-        hand_on(1, y[1])
-        minus_last = sb("minus_last", [P, PACK, 256], F32, tag="minus0")
+        for c in range(last_piece):
+            quantise_piece(c, y[c])
+        minus_last = kept("minus_last", [P, PACK, PIECES[last_piece][1]], F32, tag="minus0")
         for t in range(PACK + 1):
             if t < PACK:
-                fetch_minus(minus_last[:, t, :], t, 2)
+                fetch_subtrahend(minus_last[:, t, :], t, last_piece)
             if t > 0:
-                fetch_difference(y[2][:, t - 1, :], minus_last[:, t - 1, :], t - 1, 2)
-        hand_on(2, y[2])
-        for q in range(4):
+                fetch_difference(y[last_piece][:, t - 1, :], minus_last[:, t - 1, :], t - 1, last_piece)
+        quantise_piece(last_piece, y[last_piece])
+
+        for q in range(P // QUADRANT):
             queue = nc.scalar if q % 2 == 0 else nc.sync
             queue.dma_start(
-                out_2[0][4 * q : 4 * q + 4, :].bitcast(I32), out_scales[32 * q : 32 * q + 4, :].bitcast(I32)
+                out_2[0][4 * q : 4 * q + 4, :].bitcast(I32),
+                out_scales[QUADRANT * q : QUADRANT * q + 4, :].bitcast(I32),
             )

from contextlib import ExitStack

import concourse.mybir as mybir

K, T, S, G, H, U = 512, 1024, 512, 2048, 512, 1024
FLOPS = 2 * K * H * S + 2 * K * H * U

F32 = mybir.dt.float32
BF16 = mybir.dt.bfloat16
I32 = mybir.dt.int32
U32 = mybir.dt.uint32
U16 = mybir.dt.uint16
U8 = mybir.dt.uint8
FP8X4 = mybir.dt.float8_e4m3fn_x4
COPY = mybir.ActivationFunctionType.Copy
ADD = mybir.AluOpType.add
MULT = mybir.AluOpType.mult
SUBTRACT = mybir.AluOpType.subtract

P = 128
PACK = 4
SCALE_ROWS = 16
QUADRANT = 32
ENTRIES_PER_COLUMN = 16
BANK = 512
PSUM_BANKS = 8
LINE = 16
PAGE_BYTES = 4 * U
SIXTEENTH = 0.0625

PIECES = [(0, 512), (512, 256), (768, 256)]
LAST_ON_VECTOR = 80


def tile_picked_codepagemgap_none_po_kernel(
    tc, x_words, x_scales, d_words, d_scales, mem, gs, offs, k1, n1, n2, k2, n3, n4, out_0, out_1, out_2
):
    nc = tc.nc
    with ExitStack() as ctx:
        lists = ctx.enter_context(tc.tile_pool(name="lists", bufs=1))
        keep = ctx.enter_context(tc.tile_pool(name="keep", bufs=1))
        paged = ctx.enter_context(tc.tile_pool(name="paged", bufs=1))
        early = ctx.enter_context(tc.tile_pool(name="early", bufs=1))
        psum = ctx.enter_context(tc.psum_pool(name="psum", bufs=PSUM_BANKS))

        def kept(name, shape, dtype, tag=None):
            return keep.tile(shape, dtype, name=name, tag=tag or name, align_bytes=64)

        def placed_at(pool, offset, name, shape, dtype):
            return pool.tile(shape, dtype, name=name, align_bytes=64, offset=offset)

        def load_list(name, src):
            tile = lists.tile(list(src.shape), U16, name=name)
            nc.sync.dma_start(tile[:], src)
            return tile

        def entries(tile, start, count):
            return tile[:, start // ENTRIES_PER_COLUMN : (start + count) // ENTRIES_PER_COLUMN]

        def load_scale_rows(tile, src):
            rows = src[0].bitcast(I32)
            spread = rows.unsqueeze(1).broadcast_to([SCALE_ROWS, P // SCALE_ROWS, rows.shape[1]])
            nc.sync.dma_start(tile[:].bitcast(I32), spread)

        def load_words(dst, src):
            nc.sync.dma_start(dst.bitcast(I32), src[0].rearrange("p c r -> p (c r)").bitcast(I32))

        def move_scale_rows(queues, dst, src):
            for r in range(4):
                queues[r % len(queues)].dma_start(
                    dst[r:P:QUADRANT, :].bitcast(I32), src[8 * r : P : QUADRANT, :].bitcast(I32)
                )

        def deal(dst, src, per_line, first, count):
            nc.vector.tensor_copy(
                dst.rearrange("p (t c i) -> p c t i", t=count, i=per_line),
                src.rearrange("p (c i t) -> p c t i", t=PACK, i=per_line)[:, :, first : first + count, :],
            )

        def plane_columns(plane_0, planes_1_to_3, t):
            return plane_0[:] if t == 0 else planes_1_to_3[:, (t - 1) * P : t * P]

        def interleave(copy, dst, src):
            copy(dst.rearrange("p (c i) t -> p c t i", i=4), src.rearrange("p t (c i) -> p c t i", i=4))

        def product(width, codes, scales, moving_codes, moving_scales):
            acc = psum.tile([P, BANK], F32, name="acc", tag="acc")
            nc.tensor.matmul_mx(
                acc[:, :width],
                lhsT=codes.bitcast(FP8X4),
                lhsT_scale=scales,
                rhs=moving_codes.bitcast(FP8X4),
                rhs_scale=moving_scales,
                start=True,
                stop=True,
            )
            return acc[:, :width]

        d_scale_table = kept("d_scale_table", [P, G], U8)
        x_scale_table = kept("x_scale_table", [P, T], U8)
        x_word_span = placed_at(paged, PAGE_BYTES // 2, "x_word_span", [P, 2 * U + U // 2 + LINE], U32)
        x_word_table = x_word_span[:, :T]
        d_word_table = kept("d_word_table", [P, G], U32)

        offs_l = load_list("offs_l", offs)
        load_scale_rows(x_scale_table, x_scales)
        k1_l = load_list("k1_l", k1)
        load_scale_rows(d_scale_table, d_scales)
        k2_l = load_list("k2_l", k2)
        n1_l = load_list("n1_l", n1)
        load_words(x_word_table, x_words)
        load_words(d_word_table[:], d_words)
        n2_l = load_list("n2_l", n2)
        n4_l = load_list("n4_l", n4)
        n3_l = load_list("n3_l", n3)

        gs_t = kept("gs_t", [P, PACK], F32)
        nc.gpsimd.dma_start(gs_t[:], gs.rearrange("(p t) o -> p (t o)", t=PACK))
        gs_neg_half = kept("gs_neg_half", [P, PACK], F32)
        nc.gpsimd.tensor_scalar(gs_neg_half[:], gs_t[:], -0.5, 0.0, MULT, ADD)

        moved_b1 = kept("moved_b1", [P, H + S], U8)
        nc.vector.memset(moved_b1[:].bitcast(I32), 0)
        moved_b2 = kept("moved_b2", [P, H], U8)
        nc.vector.memset(moved_b2[:].bitcast(I32), 0)

        picked_b1 = placed_at(early, 0, "picked_b1", [P, H + S], U8)
        nc.vector.tensor_copy(picked_b1[:, H:], x_scale_table[:].indirect(offs_l[:]))
        nc.vector.tensor_copy(picked_b1[:, :H], d_scale_table[:].indirect(k1_l[:]))
        move_scale_rows([nc.scalar, nc.sync], moved_b1, picked_b1)
        x_codes = kept("x_codes", [P, S], U32)
        nc.vector.tensor_copy(x_codes[:], x_word_table.indirect(offs_l[:]))
        picked_w1 = kept("picked_w1", [P, H], U32)
        nc.vector.tensor_copy(picked_w1[:], d_word_table[:].indirect(k1_l[:]))
        w1_scales_0 = kept("w1_scales_0", [P, P], U8)
        deal(w1_scales_0[:], moved_b1[:, :H], LINE, 0, 1)
        w1_codes = placed_at(early, H, "w1_codes", [P, H], U32)
        deal(w1_codes[:, :P], picked_w1[:], LINE // 4, 0, 1)
        deal(w1_codes[:, P:], picked_w1[:], LINE // 4, 1, PACK - 1)
        w1_scales_rest = kept("w1_scales_rest", [P, (PACK - 1) * P], U8)
        deal(w1_scales_rest[:], moved_b1[:, :H], LINE, 1, PACK - 1)

        picked_b2 = placed_at(early, 0, "picked_b2", [P, H], U8)
        nc.vector.tensor_copy(picked_b2[:], d_scale_table[:].indirect(k2_l[:]))
        move_scale_rows([nc.sync], moved_b2, picked_b2)

        h = []
        for t in range(PACK):
            h_t = kept("h%d" % t, [P, S], F32)
            width = S // 2 if t == 0 else S
            for start in range(0, S, width):
                acc = product(
                    width,
                    w1_codes[:, t * P : (t + 1) * P],
                    plane_columns(w1_scales_0, w1_scales_rest, t),
                    x_codes[:, start : start + width],
                    moved_b1[:, H + start : H + start + width],
                )
                nc.scalar.activation(h_t[:, start : start + width], acc, COPY, scale=SIXTEENTH)
            h.append(h_t)

        mem_planes = mem.rearrange("(p t) w -> t p w", t=PACK)
        half = U // 2
        own, other = [], []
        for t in range(PACK):
            page = placed_at(paged, t * PAGE_BYTES, "page%d" % t, [P, U], F32)
            nc.sync.dma_start(page[:], mem_planes[t])
            nc.vector.tensor_copy(page[:].indirect(n1_l[:]), h[t][:])
            other_t = kept("other%d" % t, [P, U], F32)
            nc.scalar.activation(other_t[:], page[:], COPY, scale=gs_neg_half[:, t : t + 1])
            halves = []
            for u in range(2):
                own_tu = kept("own%d_%d" % (t, u), [P, half], F32)
                nc.scalar.activation(own_tu[:], page[:, half * u : half * (u + 1)], COPY, scale=gs_t[:, t : t + 1])
                halves.append(own_tu)
            own.append(halves)
            other.append(other_t)

        z_first = placed_at(paged, PAGE_BYTES, "z_first", [P, PACK, PIECES[0][1]], F32)
        z_rest = placed_at(paged, 3 * PAGE_BYTES, "z_rest", [P, 2 * PACK, PIECES[1][1]], F32)
        z_rounded = []
        for c, (start, width) in enumerate(PIECES):
            z = z_first[:] if c == 0 else z_rest[:, PACK * (c - 1) : PACK * c, :]
            for t in range(PACK):
                own_piece = own[t][start // half][:, start % half : start % half + width]
                nc.vector.tensor_tensor(z[:, t, :], other[t][:].indirect(entries(n2_l, start, width)), own_piece, ADD)
            z_bf16 = kept("z_bf16_%d" % c, [P, width, PACK], BF16)
            interleave(nc.scalar.copy, z_bf16[:], z)
            z_rounded.append(z_bf16)

        picked_w2 = kept("picked_w2", [P, H], U32, tag="own2_1")
        nc.vector.tensor_copy(picked_w2[:], d_word_table[:].indirect(k2_l[:]))

        z_codes, z_scales = [], []
        for c, (start, width) in enumerate(PIECES):
            codes = kept("z_codes%d" % c, [P, width], U32)
            scales = kept("z_scales%d" % c, [P, width], U8)
            nc.vector.quantize_mx(codes[:].bitcast(FP8X4), scales[:], z_rounded[c][:].rearrange("p w t -> p (w t)"))
            z_codes.append(codes)
            z_scales.append(scales)
            if c == 0:
                w2_scales_0 = kept("w2_scales_0", [P, P], U8, tag="own1_1")
                deal(w2_scales_0[:], moved_b2[:], LINE, 0, 1)
                w2_codes_0 = kept("w2_codes_0", [P, P], U32)
                deal(w2_codes_0[:], picked_w2[:], LINE // 4, 0, 1)
        w2_codes_rest = placed_at(paged, 4 * PAGE_BYTES, "w2_codes_rest", [P, (PACK - 1) * P], U32)
        deal(w2_codes_rest[:], picked_w2[:], LINE // 4, 1, PACK - 1)
        w2_scales_rest = placed_at(paged, 4 * PAGE_BYTES + PAGE_BYTES // 2, "w2_scales_rest", [P, (PACK - 1) * P], U8)
        deal(w2_scales_rest[:], moved_b2[:], LINE, 1, PACK - 1)

        last_piece = len(PIECES) - 1
        h2 = []
        for t in range(PACK):
            h2_t = kept("h2_%d" % t, [P, U], F32)
            for c, (start, width) in enumerate(PIECES):
                acc = product(
                    width,
                    plane_columns(w2_codes_0, w2_codes_rest, t),
                    plane_columns(w2_scales_0, w2_scales_rest, t),
                    z_codes[c][:],
                    z_scales[c][:],
                )
                if t == 0 and c == last_piece:
                    nc.vector.tensor_scalar_mul(h2_t[:, start : start + width], acc, SIXTEENTH)
                else:
                    nc.scalar.activation(h2_t[:, start : start + width], acc, COPY, scale=SIXTEENTH)
            h2.append(h2_t)

        out_planes = out_0.rearrange("(p t) w -> t p w", t=PACK)
        out_words = out_1[0].rearrange("p c r -> p (c r)").bitcast(I32)
        out_scales = kept("out_scales", [P, U], U8)

        def fetch_subtrahend(dst, t, c):
            nc.vector.tensor_copy(dst, h2[t][:].indirect(entries(n4_l, *PIECES[c])))

        def fetch_difference(dst, subtrahend, t, c):
            start, width = PIECES[c]
            nc.vector.tensor_tensor(dst, h2[t][:].indirect(entries(n3_l, start, width)), subtrahend, SUBTRACT)
            nc.sync.dma_start(out_planes[t][:, start : start + width], dst)

        def quantise_piece(c, y_piece):
            start, width = PIECES[c]
            y_bf16 = kept("y_bf16_%d" % c, [P, width, PACK], BF16)
            if c == last_piece:
                interleave(nc.vector.tensor_copy, y_bf16[:, :LAST_ON_VECTOR, :], y_piece[:, :, :LAST_ON_VECTOR])
                interleave(nc.scalar.copy, y_bf16[:, LAST_ON_VECTOR:, :], y_piece[:, :, LAST_ON_VECTOR:])
            else:
                interleave(nc.scalar.copy, y_bf16[:], y_piece[:])
            codes = kept("y_codes%d" % c, [P, width], U32)
            nc.vector.quantize_mx(
                codes[:].bitcast(FP8X4), out_scales[:, start : start + width], y_bf16[:].rearrange("p w t -> p (w t)")
            )
            nc.sync.dma_start(out_words[:, start : start + width], codes[:].bitcast(I32))

        y = [kept("y%d" % c, [P, PACK, width], F32) for c, (start, width) in enumerate(PIECES)]
        minus = [kept("minus%d" % c, [P, PACK, width], F32) for c, (start, width) in enumerate(PIECES[:last_piece])]
        for t in range(PACK):
            for c in range(last_piece):
                fetch_subtrahend(minus[c][:, t, :], t, c)
            for c in range(last_piece):
                fetch_difference(y[c][:, t, :], minus[c][:, t, :], t, c)
        for c in range(last_piece):
            quantise_piece(c, y[c])
        minus_last = kept("minus_last", [P, PACK, PIECES[last_piece][1]], F32, tag="minus0")
        for t in range(PACK + 1):
            if t < PACK:
                fetch_subtrahend(minus_last[:, t, :], t, last_piece)
            if t > 0:
                fetch_difference(y[last_piece][:, t - 1, :], minus_last[:, t - 1, :], t - 1, last_piece)
        quantise_piece(last_piece, y[last_piece])

        for q in range(P // QUADRANT):
            queue = nc.scalar if q % 2 == 0 else nc.sync
            queue.dma_start(
                out_2[0][4 * q : 4 * q + 4, :].bitcast(I32),
                out_scales[QUADRANT * q : QUADRANT * q + 4, :].bitcast(I32),
            )
